import numpy as np
import ml_dtypes


def mxq(x, axis, fmt="e4m3"):
    dtype, down = {"e4m3": (ml_dtypes.float8_e4m3fn, 7), "e5m2": (ml_dtypes.float8_e5m2, 14)}[fmt]
    v = np.moveaxis(np.asarray(x, np.float32).astype(ml_dtypes.bfloat16).astype(np.float64), axis, -1)
    blocks = v.reshape(v.shape[:-1] + (-1, 32))
    amax = np.abs(blocks).max(-1, keepdims=True)
    byte = np.maximum(np.where(amax > 0, np.frexp(amax)[1] - 1 + 127, 0) - down, 1)
    scale = np.exp2(byte - 127.0)
    codes = (blocks / scale).astype(np.float32).astype(dtype).astype(np.float64)
    return np.moveaxis((codes * scale).reshape(v.shape), -1, axis)


WIDE = False


def mx_kscale(k):
    if not WIDE:
        return np.ones(k)
    levels = np.array([30, -30])
    if k % 512:
        return np.exp2(np.random.permutation(np.resize(levels, k // 32))).repeat(32)
    a = np.empty((k // 512, 16))
    for p in range(k // 512):
        a[p, :8] = np.random.permutation(np.resize(levels, 8))
        for g in range(8):
            far = levels[np.abs(levels - a[p, g]) >= 10]
            a[p, g + 8] = far[np.random.randint(len(far))]
    return np.exp2(a.ravel()).repeat(32)


def f64(x):
    return np.asarray(x).astype(np.float64)


def striped(idx):
    return np.tile(idx.reshape(-1, 16).T, (8, 1)).astype(np.uint16)


def unstriped(offs):
    return offs[:16].T.reshape(-1).astype(np.int64)


E2M1 = np.array([0.0, 0.5, 1.0, 1.5, 2.0, 3.0, 4.0, 6.0, -0.0, -0.5, -1.0, -1.5, -2.0, -3.0, -4.0, -6.0])


def pack_weight(w, fmt):
    k, n = w.shape
    w = f64(np.asarray(w, np.float32).astype(ml_dtypes.bfloat16)).reshape(k // 32, 32, n)
    amax = np.abs(w).max(1)
    if fmt == "e4m3":
        byte = np.frexp(amax)[1] - 1 + 127 - 7
    else:
        mant, ex = np.frexp(amax / 6.0)
        byte = np.where(mant > 0.5, ex, ex - 1) + 127
    byte = np.clip(np.where(amax > 0, byte, 1), 1, 254)
    scaled = (w * np.exp2(127.0 - byte)[:, None, :]).reshape(k, n).astype(np.float32)
    by_word = np.ascontiguousarray(scaled.reshape(k // 512, 128, 4, n).transpose(0, 1, 3, 2))
    if fmt == "e4m3":
        words = by_word.astype(ml_dtypes.float8_e4m3fn).view(np.uint8)
    else:
        c = by_word.astype(ml_dtypes.float4_e2m1fn).view(np.uint8) & 0xF
        words = (c[..., 0::2] | (c[..., 1::2] << 4)).reshape(k // 512, 128, 2 * n)
    return np.ascontiguousarray(words), np.ascontiguousarray(byte.astype(np.uint8).reshape(k // 512, 16, n))


def unpack_weight(words, scales, fmt):
    g, _, n = scales.shape
    words = np.ascontiguousarray(words).reshape(g, 128, n, -1)
    if fmt == "e4m3":
        vals = words.view(ml_dtypes.float8_e4m3fn).astype(np.float64)
    else:
        nib = np.empty((g, 128, n, 4), np.uint8)
        nib[..., 0::2] = words & 0xF
        nib[..., 1::2] = words >> 4
        vals = E2M1[nib]
    vals = vals * np.repeat(np.exp2(scales.astype(np.float64) - 127.0), 8, axis=1)[..., None]
    return vals.transpose(0, 1, 3, 2).reshape(g * 512, n)


def d_silu(v):
    s = 1.0 / (1.0 + np.exp(-np.maximum(v, -700.0)))
    return s * (1.0 + v * (1.0 - s))


K, T, E, C, H, N = 256, 1536, 6, 512, 1024, 512


def by_expert(wq, xq):
    return np.concatenate([wq[e].T @ xq[:, e * C:(e + 1) * C] for e in range(E)], axis=1)


def setup_inputs():
    n = np.random.standard_normal
    s = mx_kscale(N)[:, None]
    u = mx_kscale(H)
    first = np.random.permutation(np.repeat(np.arange(E), T // E))
    second = (first + 1 + np.random.permutation(np.repeat(np.arange(E - 1), -(-T // (E - 1)))[:T])) % E
    while np.bincount(second, minlength=E).max() != T // E:
        load = np.bincount(second, minlength=E); hi, lo = int(load.argmax()), int(load.argmin())
        t = np.flatnonzero((second == hi) & (first != lo))[0]; second[t] = lo
    slot_token = np.empty(E * C, np.int64); pos = np.empty((2, T), np.int64); fill = np.zeros(E, np.int64)
    place = np.stack([np.random.permutation(C) for _ in range(E)])
    for r, deal in enumerate((first, second)):
        for t in np.random.permutation(T):
            e = deal[t]; j = e * C + place[e, fill[e]]; fill[e] += 1; slot_token[j] = t; pos[r, t] = j
    g = np.random.uniform(0.2, 0.8, T)
    w_slot = np.empty(E * C); w_slot[pos[0]] = g; w_slot[pos[1]] = 1.0 - g
    w2 = [pack_weight(m, "e2m1") for m in n((E, N, H)) / np.sqrt(N) / s[None] * u[None, None, :]]
    w1 = [pack_weight(m, "e2m1") for m in n((E, H, K)) / np.sqrt(H) / u[None, :, None]]
    return {
        "dyT": (n((N, T)) * s).astype(np.float32),
        "a": n((H, E * C)).astype(np.float32),
        "w2_words": np.stack([m[0] for m in w2]),
        "w2_scales": np.stack([m[1] for m in w2]),
        "w1_words": np.stack([m[0] for m in w1]),
        "w1_scales": np.stack([m[1] for m in w1]),
        "gate": np.tile(w_slot, (N, 1)).astype(np.float32),
        "offs": striped(slot_token),
        "pos1": striped(pos[0]),
        "pos2": striped(pos[1]),
    }


def reference(dyT, a, w2_words, w2_scales, w1_words, w1_scales, gate, offs, pos1, pos2):
    idx = unstriped(offs)
    w2 = np.stack([unpack_weight(w2_words[e], w2_scales[e], "e2m1") for e in range(E)])
    w1 = np.stack([unpack_weight(w1_words[e], w1_scales[e], "e2m1") for e in range(E)])
    gq = mxq(f64(gate) * f64(dyT)[:, idx], 0, "e5m2")
    dh = by_expert(w2, gq)
    da = dh * d_silu(f64(a))
    dx = by_expert(w1, mxq(da, 0, "e5m2"))
    return dx[:, unstriped(pos1)] + dx[:, unstriped(pos2)]

@@ -1,0 +1,269 @@
+from contextlib import ExitStack
+
+import concourse.mybir as mybir
+from concourse.masks import make_identity
+
+K, T, E, C, H, N = 256, 1536, 6, 512, 1024, 512
+S = E * C
+FLOPS = 2 * S * N * H + 2 * S * H * K
+BYTES = 4 * (N * T + H * S + 128 * S + K * T) + E * (N * H // 2 + N * H // 32 + H * K // 2 + H * K // 32) + 2 * 128 * (S + 2 * T) // 16
+
+F32 = mybir.dt.float32
+BF16 = mybir.dt.bfloat16
+I32 = mybir.dt.int32
+U32 = mybir.dt.uint32
+U16 = mybir.dt.uint16
+U8 = mybir.dt.uint8
+E5X4 = mybir.dt.float8_e5m2_x4
+E2X4 = mybir.dt.float4_e2m1fn_x4
+MULT, ADD, SUB = mybir.AluOpType.mult, mybir.AluOpType.add, mybir.AluOpType.subtract
+TANH = mybir.ActivationFunctionType.Tanh
+SILU = mybir.ActivationFunctionType.Silu
+COPY = mybir.ActivationFunctionType.Copy
+
+P = 128
+TILES = S // P
+PER = C // P
+
+
+def tile_moe_bdx_mlp_silu_kernel(
+    tc, dyT, a, w2_words, w2_scales, w1_words, w1_scales, gate, offs, pos1, pos2, out
+):
+    nc = tc.nc
+    with ExitStack() as ctx:
+        held = ctx.enter_context(tc.tile_pool(name="held", bufs=1))
+        ring2 = ctx.enter_context(tc.tile_pool(name="ring2", bufs=2))
+        ring3 = ctx.enter_context(tc.tile_pool(name="ring3", bufs=3))
+        ring4 = ctx.enter_context(tc.tile_pool(name="ring4", bufs=4))
+        ps_a = ctx.enter_context(tc.psum_pool(name="ps_a", bufs=3))
+        ps_h = ctx.enter_context(tc.psum_pool(name="ps_h", bufs=2))
+        ps_t = ctx.enter_context(tc.psum_pool(name="ps_t", bufs=1))
+        ps_x = ctx.enter_context(tc.psum_pool(name="ps_x", bufs=2))
+
+        offsets = held.tile([P, S // 16], U16, name="offsets")
+        nc.sync.dma_start(offsets[:], offs)
+        warm = held.tile([P, 8], F32, name="warm")
+        nc.vector.memset(warm[:], 0.0)
+        nc.scalar.activation(warm[:], warm[:], SILU)
+        w2s = held.tile([P, E, H], U8, name="w2s", align_bytes=64)
+        w1s = held.tile([P, E * 2, K], U8, name="w1s", align_bytes=64)
+        nc.vector.memset(w2s[:].bitcast(I32), 0)
+        nc.vector.memset(w1s[:].bitcast(I32), 0)
+        ident = held.tile([P, P], F32, name="ident")
+        make_identity(nc, ident[:])
+
+        dy_rows = dyT.rearrange("(p j) t -> p j t", j=4)
+        a_rows = a.rearrange("(b p) s -> p b s", p=P)
+        dy = []
+        gates = []
+        a_tiles = {}
+
+        def load_gate(q):
+            tile = held.tile([P, 2 * C], F32, name="gate%d" % q)
+            nc.sync.dma_start(tile[:], gate[0:P, q * 2 * C : (q + 1) * 2 * C])
+            gates.append(tile)
+
+        def load_a(h):
+            tile = ring4.tile([P, 8, 2 * P], F32, name="a_half")
+            nc.sync.dma_start(tile[:], a_rows[:, :, h * 2 * P : (h + 1) * 2 * P])
+            a_tiles[h] = tile
+
+        w2 = []
+
+        def load_w2(e):
+            tile = held.tile([P, 2 * H], U8, name="w2_%d" % e, align_bytes=64)
+            nc.sync.dma_start(tile[:].bitcast(I32), w2_words[e, 0].bitcast(I32))
+            w2.append(tile)
+
+        for j in range(4):
+            plane = held.tile([P, T], F32, name="dy%d" % j, tag="plane%d" % j)
+            nc.sync.dma_start(plane[:], dy_rows[:, j, :])
+            dy.append(plane)
+            if j == 0:
+                load_gate(0)
+        load_a(0)
+        w2s_rows = w2_scales.rearrange("e s f i -> f (e s) i").bitcast(I32)
+        w1s_rows = w1_scales.rearrange("e s f k -> f (e s) k").bitcast(I32)
+        for q in range(4):
+            nc.scalar.dma_start(w2s[32 * q : 32 * q + 4].bitcast(I32), w2s_rows[4 * q : 4 * q + 4])
+        for q in range(4):
+            nc.scalar.dma_start(w1s[32 * q : 32 * q + 4].bitcast(I32), w1s_rows[4 * q : 4 * q + 4])
+        load_w2(0)
+        load_a(1)
+        load_gate(1)
+        load_a(2)
+        load_w2(1)
+        w1 = held.tile([P, E * 2, 2 * K], U8, name="w1", align_bytes=64)
+        nc.sync.dma_start(w1[:].bitcast(I32), w1_words.rearrange("e s p k -> p (e s) k").bitcast(I32))
+        load_a(3)
+        load_gate(2)
+        for e in range(2, E):
+            load_w2(e)
+        first = held.tile([P, T // 16], U16, name="first")
+        nc.sync.dma_start(first[:], pos1)
+        second = held.tile([P, T // 16], U16, name="second")
+        nc.sync.dma_start(second[:], pos2)
+
+        dx = [held.tile([P, S], F32, name="dx%d" % m) for m in range(2)]
+
+        g4 = {}
+        pairs = {}
+        g_bf = {}
+        g_codes = {}
+        g_scales = {}
+
+        def gather(e, j, experts):
+            if e % 2 == 0 and j == 0:
+                pair = ring2.tile([P, 4, 2 * C], F32, name="g4")
+                g4[e] = pair[:, :, 0:C]
+                g4[e + 1] = pair[:, :, C : 2 * C]
+                pairs[e // 2] = pair
+            lo = (e % 2) * C
+            hi = lo + experts * C
+            nc.vector.tensor_tensor(
+                pairs[e // 2][:, j, lo:hi],
+                dy[j][:].indirect(offsets[:, e * (C // 16) : (e + experts) * (C // 16)]),
+                gates[e // 2][:, lo:hi],
+                MULT,
+            )
+
+        def interleave(e):
+            tile = ring2.tile([P, 4 * C], BF16, name="g_bf", align_bytes=64)
+            nc.scalar.copy(
+                tile[:].rearrange("p (c i t) -> p c t i", i=4, t=4),
+                g4[e].rearrange("p t (c i) -> p c t i", i=4),
+            )
+            g_bf[e] = tile
+
+        def quantise_g(e):
+            codes = ring2.tile([P, C], U32, name="g_codes", align_bytes=64)
+            scales = ring2.tile([P, C], U8, name="g_scales", align_bytes=64)
+            nc.vector.quantize_mx(out=codes[:].bitcast(E5X4), scales=scales[:], in_=g_bf[e][:])
+            g_codes[e], g_scales[e] = codes, scales
+
+        th = {}
+        w = {}
+
+        def saved(i):
+            th[i] = ring3.tile([P, H], F32, name="th")
+            w[i] = ring3.tile([P, H], F32, name="w")
+            col = (i % 2) * P
+            for half in range(2):
+                bank = ps_a.tile([P, 512], F32, name="aT")
+                for b in range(4):
+                    nc.tensor.transpose(bank[:, b * P : (b + 1) * P], a_tiles[i // 2][:, half * 4 + b, col : col + P], ident[:])
+                nc.scalar.activation(th[i][:, half * 512 : (half + 1) * 512], bank[:], TANH, scale=0.5)
+                nc.scalar.activation(w[i][:, half * 512 : (half + 1) * 512], bank[:], SILU, scale=-1.0)
+
+        da = {}
+
+        def hidden(i):
+            e, c = i // PER, i % PER
+            y = ring2.tile([P, H], F32, name="y")
+            for half in range(2):
+                bank = ps_h.tile([P, 512], F32, name="dh")
+                nc.tensor.matmul_mx(
+                    out=bank[:],
+                    lhsT=g_codes[e][:, c * P : (c + 1) * P].bitcast(E5X4),
+                    lhsT_scale=g_scales[e][:, c * P : (c + 1) * P],
+                    rhs=w2[e][:, half * 1024 : (half + 1) * 1024].bitcast(E2X4),
+                    rhs_scale=w2s[:, e, half * 512 : (half + 1) * 512],
+                    start=True,
+                    stop=True,
+                )
+                cols = slice(half * 512, (half + 1) * 512)
+                nc.vector.scalar_tensor_tensor(out=y[:, cols], in0=w[i][:, cols], scalar=1.0, in1=bank[:], op0=SUB, op1=MULT)
+            da[i] = ring2.tile([P, H], BF16, name="da", align_bytes=64)
+            nc.vector.scalar_tensor_tensor(out=da[i][:], in0=th[i][:], scalar=1.0, in1=y[:], op0=ADD, op1=MULT)
+
+        da_t = {}
+
+        def turn(i):
+            e, c = i // PER, i % PER
+            if c == 0:
+                da_t[e] = ring2.tile([P, 2, 4 * C], BF16, name="da_t", align_bytes=64)
+            words = da[i][:].bitcast(F32)
+            bank = ps_t.tile([P, 512], F32, name="daT")
+            for g in range(2):
+                for u in range(2):
+                    q = 2 * g + u
+                    nc.tensor.transpose(bank[:, q * P : (q + 1) * P], words[:, 256 * g + u : 256 * (g + 1) : 2], ident[:])
+            nc.scalar.copy(
+                da_t[e][:].bitcast(F32).rearrange("p g (s u) -> p g s u", u=2)[:, :, c * P : (c + 1) * P, :],
+                bank[:].rearrange("p (g u s) -> p g s u", g=2, u=2),
+            )
+
+        d_codes = {}
+        d_scales = {}
+
+        def quantise_da(e, lo, hi):
+            if lo == 0:
+                d_codes[e] = ring2.tile([P, 2, C], U32, name="d_codes", align_bytes=64)
+                d_scales[e] = ring2.tile([P, 2, C], U8, name="d_scales", align_bytes=64)
+            cols = slice(lo * P, hi * P)
+            for g in range(2):
+                nc.vector.quantize_mx(
+                    out=d_codes[e][:, g, cols].bitcast(E5X4),
+                    scales=d_scales[e][:, g, cols],
+                    in_=da_t[e][:, g, lo * 512 : hi * 512],
+                )
+
+        def product(e):
+            for m in range(2):
+                bank = ps_x.tile([P, C], F32, name="dxT")
+                for g in range(2):
+                    nc.tensor.matmul_mx(
+                        out=bank[:],
+                        lhsT=w1[:, 2 * e + g, m * 256 : (m + 1) * 256].bitcast(E2X4),
+                        lhsT_scale=w1s[:, 2 * e + g, m * P : (m + 1) * P],
+                        rhs=d_codes[e][:, g, :].bitcast(E5X4),
+                        rhs_scale=d_scales[e][:, g, :],
+                        start=(g == 0),
+                        stop=(g == 1),
+                    )
+                nc.scalar.activation(dx[m][:, e * C : (e + 1) * C], bank[:], COPY, scale=-0.5)
+
+        for e in range(2):
+            for j in range(4):
+                gather(e, j, 1)
+        interleave(0)
+        saved(0)
+        quantise_g(0)
+        saved(1)
+        for i in range(TILES):
+            e, c = i // PER, i % PER
+            if i + 2 < TILES:
+                if (i + 2) % 2 == 0 and (i + 2) // 2 + 2 < TILES // 2 and (i + 2) // 2 + 2 not in a_tiles:
+                    load_a((i + 2) // 2 + 2)
+                saved(i + 2)
+            if e % 2 == 0 and e + 2 < E:
+                gather(e + 2, c, 2)
+            if c == 0 and e + 1 < E:
+                interleave(e + 1)
+            if c == 2 and e + 1 < E:
+                quantise_g(e + 1)
+            hidden(i)
+            if i >= 1:
+                turn(i - 1)
+            if i >= 2 and (i - 2) % PER == PER - 1:
+                done = (i - 2) // PER
+                quantise_da(done, 0, PER)
+                product(done)
+            if i == TILES - 1:
+                quantise_da(E - 1, 0, 2)
+        turn(TILES - 1)
+        quantise_da(E - 1, 2, 4)
+        product(E - 1)
+
+        for m in range(2):
+            one = held.tile([P, T], F32, name="one%d" % m, tag="plane%d" % (2 * m))
+            two = held.tile([P, T], F32, name="two%d" % m, tag="plane%d" % (2 * m + 1))
+            for h in range(2):
+                cols = slice(h * 768, (h + 1) * 768)
+                lists = slice(h * 48, (h + 1) * 48)
+                nc.vector.tensor_copy(one[:, cols], dx[m][:].indirect(first[:, lists]))
+                nc.vector.tensor_copy(two[:, cols], dx[m][:].indirect(second[:, lists]))
+                total = ring2.tile([P, 768], F32, name="total")
+                adder = nc.gpsimd if m == 0 else nc.vector
+                adder.tensor_tensor(total[:], one[:, cols], two[:, cols], ADD)
+                nc.sync.dma_start(out[m * P : (m + 1) * P, cols], total[:])

@@ -32,13 +32,15 @@ def tile_moe_bdx_mlp_silu_kernel(
     nc = tc.nc
     with ExitStack() as ctx:
         held = ctx.enter_context(tc.tile_pool(name="held", bufs=1))
+        ring_a = ctx.enter_context(tc.tile_pool(name="ring_a", bufs=3))
+        ring_s = ctx.enter_context(tc.tile_pool(name="ring_s", bufs=5))
         ring2 = ctx.enter_context(tc.tile_pool(name="ring2", bufs=2))
         ring3 = ctx.enter_context(tc.tile_pool(name="ring3", bufs=3))
         ring4 = ctx.enter_context(tc.tile_pool(name="ring4", bufs=4))
-        ps_a = ctx.enter_context(tc.psum_pool(name="ps_a", bufs=3))
-        ps_h = ctx.enter_context(tc.psum_pool(name="ps_h", bufs=2))
-        ps_t = ctx.enter_context(tc.psum_pool(name="ps_t", bufs=1))
-        ps_x = ctx.enter_context(tc.psum_pool(name="ps_x", bufs=2))
+        ps_a = ctx.enter_context(tc.psum_pool(name="ps_a", bufs=2))
+        ps_h = ctx.enter_context(tc.psum_pool(name="ps_h", bufs=3))
+        ps_t = ctx.enter_context(tc.psum_pool(name="ps_t", bufs=2))
+        ps_x = ctx.enter_context(tc.psum_pool(name="ps_x", bufs=1))
 
         offsets = held.tile([P, S // 16], U16, name="offsets")
         nc.sync.dma_start(offsets[:], offs)
@@ -47,58 +49,75 @@ def tile_moe_bdx_mlp_silu_kernel(
         nc.scalar.activation(warm[:], warm[:], SILU)
         w2s = held.tile([P, E, H], U8, name="w2s", align_bytes=64)
         w1s = held.tile([P, E * 2, K], U8, name="w1s", align_bytes=64)
-        nc.vector.memset(w2s[:].bitcast(I32), 0)
-        nc.vector.memset(w1s[:].bitcast(I32), 0)
+        nc.gpsimd.memset(w2s[:].bitcast(I32), 0)
+        nc.gpsimd.memset(w1s[:].bitcast(I32), 0)
         ident = held.tile([P, P], F32, name="ident")
         make_identity(nc, ident[:])
 
         dy_rows = dyT.rearrange("(p j) t -> p j t", j=4)
         a_rows = a.rearrange("(b p) s -> p b s", p=P)
-        dy = []
-        gates = []
-        a_tiles = {}
-
-        def load_gate(q):
-            tile = held.tile([P, 2 * C], F32, name="gate%d" % q)
-            nc.sync.dma_start(tile[:], gate[0:P, q * 2 * C : (q + 1) * 2 * C])
-            gates.append(tile)
-
-        def load_a(h):
-            tile = ring4.tile([P, 8, 2 * P], F32, name="a_half")
-            nc.sync.dma_start(tile[:], a_rows[:, :, h * 2 * P : (h + 1) * 2 * P])
-            a_tiles[h] = tile
-
-        w2 = []
-
-        def load_w2(e):
-            tile = held.tile([P, 2 * H], U8, name="w2_%d" % e, align_bytes=64)
-            nc.sync.dma_start(tile[:].bitcast(I32), w2_words[e, 0].bitcast(I32))
-            w2.append(tile)
-
-        for j in range(4):
-            plane = held.tile([P, T], F32, name="dy%d" % j, tag="plane%d" % j)
-            nc.sync.dma_start(plane[:], dy_rows[:, j, :])
-            dy.append(plane)
-            if j == 0:
-                load_gate(0)
-        load_a(0)
         w2s_rows = w2_scales.rearrange("e s f i -> f (e s) i").bitcast(I32)
         w1s_rows = w1_scales.rearrange("e s f k -> f (e s) k").bitcast(I32)
-        for q in range(4):
-            nc.scalar.dma_start(w2s[32 * q : 32 * q + 4].bitcast(I32), w2s_rows[4 * q : 4 * q + 4])
-        for q in range(4):
-            nc.scalar.dma_start(w1s[32 * q : 32 * q + 4].bitcast(I32), w1s_rows[4 * q : 4 * q + 4])
-        load_w2(0)
-        load_a(1)
+        dy = {}
+        gates = {}
+        a_tiles = {}
+        w2 = {}
+
+        def load_gate(e):
+            gates[e] = held.tile([P, C], F32, name="gate%d" % e)
+            nc.sync.dma_start(gates[e][:], gate[0:P, e * C : (e + 1) * C])
+
+        def load_dy(j):
+            dy[j] = held.tile([P, T], F32, name="dy%d" % j, tag="plane%d" % j)
+            nc.sync.dma_start(dy[j][:], dy_rows[:, j, :])
+
+        def load_a(h):
+            if 2 * h in a_tiles or h >= TILES // 2:
+                return
+            tile = ring_a.tile([P, 8, 2 * P], F32, name="a_half")
+            nc.sync.dma_start(tile[:], a_rows[:, :, h * 2 * P : (h + 1) * 2 * P])
+            a_tiles[2 * h] = tile[:, :, 0:P]
+            a_tiles[2 * h + 1] = tile[:, :, P : 2 * P]
+
+        def load_a_tile(i):
+            tile = held.tile([P, 8, P], F32, name="a_tile%d" % i)
+            nc.sync.dma_start(tile[:], a_rows[:, :, i * P : (i + 1) * P])
+            a_tiles[i] = tile[:]
+
+        def load_w2(e):
+            w2[e] = held.tile([P, 2 * H], U8, name="w2_%d" % e, align_bytes=64)
+            nc.sync.dma_start(w2[e][:].bitcast(I32), w2_words[e, 0].bitcast(I32))
+
+        def load_w2s():
+            for q in range(4):
+                nc.sync.dma_start(w2s[32 * q : 32 * q + 4].bitcast(I32), w2s_rows[4 * q : 4 * q + 4])
+
+        def load_w1s():
+            for q in range(4):
+                nc.sync.dma_start(w1s[32 * q : 32 * q + 4].bitcast(I32), w1s_rows[4 * q : 4 * q + 4])
+
+        load_gate(0)
+        load_dy(0)
         load_gate(1)
-        load_a(2)
+        load_dy(1)
+        load_a_tile(0)
+        load_dy(2)
+        load_dy(3)
+        load_w2s()
+        load_w2(0)
+        load_a_tile(1)
+        load_a(1)
         load_w2(1)
+        load_a(2)
+        load_w1s()
+        load_a(3)
         w1 = held.tile([P, E * 2, 2 * K], U8, name="w1", align_bytes=64)
         nc.sync.dma_start(w1[:].bitcast(I32), w1_words.rearrange("e s p k -> p (e s) k").bitcast(I32))
-        load_a(3)
-        load_gate(2)
-        for e in range(2, E):
-            load_w2(e)
+        for e in range(E):
+            if e not in w2:
+                load_w2(e)
+            if e not in gates:
+                load_gate(e)
         first = held.tile([P, T // 16], U16, name="first")
         nc.sync.dma_start(first[:], pos1)
         second = held.tile([P, T // 16], U16, name="second")
@@ -107,61 +126,62 @@ def tile_moe_bdx_mlp_silu_kernel(
         dx = [held.tile([P, S], F32, name="dx%d" % m) for m in range(2)]
 
         g4 = {}
-        pairs = {}
         g_bf = {}
         g_codes = {}
         g_scales = {}
 
-        def gather(e, j, experts):
-            if e % 2 == 0 and j == 0:
-                pair = ring2.tile([P, 4, 2 * C], F32, name="g4")
-                g4[e] = pair[:, :, 0:C]
-                g4[e + 1] = pair[:, :, C : 2 * C]
-                pairs[e // 2] = pair
-            lo = (e % 2) * C
-            hi = lo + experts * C
+        def gather(e, j):
+            if j == 0:
+                g4[e] = ring2.tile([P, 4, C], F32, name="g4")
             nc.vector.tensor_tensor(
-                pairs[e // 2][:, j, lo:hi],
-                dy[j][:].indirect(offsets[:, e * (C // 16) : (e + experts) * (C // 16)]),
-                gates[e // 2][:, lo:hi],
+                g4[e][:, j, :],
+                dy[j][:].indirect(offsets[:, e * (C // 16) : (e + 1) * (C // 16)]),
+                gates[e][:],
                 MULT,
             )
 
-        def interleave(e):
-            tile = ring2.tile([P, 4 * C], BF16, name="g_bf", align_bytes=64)
+        def interleave(e, lo, hi):
+            if lo == 0:
+                g_bf[e] = ring2.tile([P, 4 * C], BF16, name="g_bf", align_bytes=64)
             nc.scalar.copy(
-                tile[:].rearrange("p (c i t) -> p c t i", i=4, t=4),
-                g4[e].rearrange("p t (c i) -> p c t i", i=4),
+                g_bf[e][:, 4 * lo : 4 * hi].rearrange("p (c i t) -> p c t i", i=4, t=4),
+                g4[e][:, :, lo:hi].rearrange("p t (c i) -> p c t i", i=4),
             )
-            g_bf[e] = tile
 
-        def quantise_g(e):
-            codes = ring2.tile([P, C], U32, name="g_codes", align_bytes=64)
-            scales = ring2.tile([P, C], U8, name="g_scales", align_bytes=64)
-            nc.vector.quantize_mx(out=codes[:].bitcast(E5X4), scales=scales[:], in_=g_bf[e][:])
-            g_codes[e], g_scales[e] = codes, scales
+        def quantise_g(e, lo, hi):
+            if lo == 0:
+                g_codes[e] = ring2.tile([P, C], U32, name="g_codes", align_bytes=64)
+                g_scales[e] = ring2.tile([P, C], U8, name="g_scales", align_bytes=64)
+            nc.vector.quantize_mx(out=g_codes[e][:, lo:hi].bitcast(E5X4), scales=g_scales[e][:, lo:hi], in_=g_bf[e][:, 4 * lo : 4 * hi])
 
         th = {}
         w = {}
 
         def saved(i):
-            th[i] = ring3.tile([P, H], F32, name="th")
-            w[i] = ring3.tile([P, H], F32, name="w")
-            col = (i % 2) * P
+            if i >= TILES:
+                return
+            th[i] = ring_s.tile([P, H], F32, name="th")
+            w[i] = ring_s.tile([P, H], F32, name="w")
             for half in range(2):
+                cols = slice(half * 512, (half + 1) * 512)
                 bank = ps_a.tile([P, 512], F32, name="aT")
                 for b in range(4):
-                    nc.tensor.transpose(bank[:, b * P : (b + 1) * P], a_tiles[i // 2][:, half * 4 + b, col : col + P], ident[:])
-                nc.scalar.activation(th[i][:, half * 512 : (half + 1) * 512], bank[:], TANH, scale=0.5)
-                nc.scalar.activation(w[i][:, half * 512 : (half + 1) * 512], bank[:], SILU, scale=-1.0)
+                    nc.tensor.transpose(bank[:, b * P : (b + 1) * P], a_tiles[i][:, half * 4 + b, :], ident[:])
+                nc.scalar.activation(w[i][:, cols], bank[:], SILU, scale=-1.0)
+                nc.scalar.activation(th[i][:, cols], bank[:], TANH, scale=0.5)
 
         da = {}
+        y = {}
+        dh = {}
 
         def hidden(i):
+            if i >= TILES:
+                return
             e, c = i // PER, i % PER
-            y = ring2.tile([P, H], F32, name="y")
+            dh[i] = []
             for half in range(2):
                 bank = ps_h.tile([P, 512], F32, name="dh")
+                dh[i].append(bank)
                 nc.tensor.matmul_mx(
                     out=bank[:],
                     lhsT=g_codes[e][:, c * P : (c + 1) * P].bitcast(E5X4),
@@ -171,41 +191,55 @@ def tile_moe_bdx_mlp_silu_kernel(
                     start=True,
                     stop=True,
                 )
+
+        def first_product(i):
+            if i >= TILES:
+                return
+            y[i] = ring2.tile([P, H], F32, name="y")
+            for half in range(2):
                 cols = slice(half * 512, (half + 1) * 512)
-                nc.vector.scalar_tensor_tensor(out=y[:, cols], in0=w[i][:, cols], scalar=1.0, in1=bank[:], op0=SUB, op1=MULT)
-            da[i] = ring2.tile([P, H], BF16, name="da", align_bytes=64)
-            nc.vector.scalar_tensor_tensor(out=da[i][:], in0=th[i][:], scalar=1.0, in1=y[:], op0=ADD, op1=MULT)
+                nc.vector.scalar_tensor_tensor(out=y[i][:, cols], in0=w[i][:, cols], scalar=1.0, in1=dh[i][half][:], op0=SUB, op1=MULT)
+
+        def second_product(i):
+            if not 0 <= i < TILES:
+                return
+            da[i] = ring4.tile([P, H], BF16, name="da", align_bytes=64)
+            nc.vector.scalar_tensor_tensor(out=da[i][:], in0=th[i][:], scalar=1.0, in1=y[i][:], op0=ADD, op1=MULT)
 
         da_t = {}
 
         def turn(i):
-            e, c = i // PER, i % PER
-            if c == 0:
-                da_t[e] = ring2.tile([P, 2, 4 * C], BF16, name="da_t", align_bytes=64)
+            if not 0 <= i < TILES:
+                return
+            if i % 2 == 0:
+                da_t[i // 2] = ring3.tile([P, 2, 8 * P], BF16, name="da_t", align_bytes=64)
             words = da[i][:].bitcast(F32)
             bank = ps_t.tile([P, 512], F32, name="daT")
             for g in range(2):
                 for u in range(2):
                     q = 2 * g + u
                     nc.tensor.transpose(bank[:, q * P : (q + 1) * P], words[:, 256 * g + u : 256 * (g + 1) : 2], ident[:])
+            half = (i % 2) * P
             nc.scalar.copy(
-                da_t[e][:].bitcast(F32).rearrange("p g (s u) -> p g s u", u=2)[:, :, c * P : (c + 1) * P, :],
+                da_t[i // 2][:].bitcast(F32).rearrange("p g (s u) -> p g s u", u=2)[:, :, half : half + P, :],
                 bank[:].rearrange("p (g u s) -> p g s u", g=2, u=2),
             )
 
         d_codes = {}
         d_scales = {}
 
-        def quantise_da(e, lo, hi):
-            if lo == 0:
+        def quantise_da(i, tiles):
+            e, c = i // PER, i % PER
+            if c == 0:
                 d_codes[e] = ring2.tile([P, 2, C], U32, name="d_codes", align_bytes=64)
                 d_scales[e] = ring2.tile([P, 2, C], U8, name="d_scales", align_bytes=64)
-            cols = slice(lo * P, hi * P)
+            cols = slice(c * P, (c + tiles) * P)
+            half = (i % 2) * P
             for g in range(2):
                 nc.vector.quantize_mx(
                     out=d_codes[e][:, g, cols].bitcast(E5X4),
                     scales=d_scales[e][:, g, cols],
-                    in_=da_t[e][:, g, lo * 512 : hi * 512],
+                    in_=da_t[i // 2][:, g, 4 * half : 4 * (half + tiles * P)],
                 )
 
         def product(e):
@@ -223,47 +257,52 @@ def tile_moe_bdx_mlp_silu_kernel(
                     )
                 nc.scalar.activation(dx[m][:, e * C : (e + 1) * C], bank[:], COPY, scale=-0.5)
 
-        for e in range(2):
-            for j in range(4):
-                gather(e, j, 1)
-        interleave(0)
+        for j in range(4):
+            gather(0, j)
+        for q in range(4):
+            interleave(0, q * P, (q + 1) * P)
+            quantise_g(0, q * P, (q + 1) * P)
         saved(0)
-        quantise_g(0)
-        saved(1)
-        for i in range(TILES):
+        hidden(0)
+        for i in range(1, 3):
+            saved(i)
+        for i in range(TILES + 2):
             e, c = i // PER, i % PER
-            if i + 2 < TILES:
-                if (i + 2) % 2 == 0 and (i + 2) // 2 + 2 < TILES // 2 and (i + 2) // 2 + 2 not in a_tiles:
-                    load_a((i + 2) // 2 + 2)
-                saved(i + 2)
-            if e % 2 == 0 and e + 2 < E:
-                gather(e + 2, c, 2)
-            if c == 0 and e + 1 < E:
-                interleave(e + 1)
-            if c == 2 and e + 1 < E:
-                quantise_g(e + 1)
-            hidden(i)
-            if i >= 1:
-                turn(i - 1)
-            if i >= 2 and (i - 2) % PER == PER - 1:
-                done = (i - 2) // PER
-                quantise_da(done, 0, PER)
-                product(done)
-            if i == TILES - 1:
-                quantise_da(E - 1, 0, 2)
-        turn(TILES - 1)
-        quantise_da(E - 1, 2, 4)
+            turn(i - 2)
+            load_a((i + 1) // 2 + 3)
+            saved(i + 3)
+            first_product(i)
+            second_product(i - 1)
+            if e + 1 < E:
+                if c == 0:
+                    gather(e + 1, 0)
+                    gather(e + 1, 1)
+                elif c <= 2:
+                    gather(e + 1, c + 1)
+                if c >= 2:
+                    interleave(e + 1, (c - 2) * 256, (c - 1) * 256)
+                if c == 3:
+                    quantise_g(e + 1, 0, 256)
+                    quantise_g(e + 1, 256, 512)
+            hidden(i + 1)
+            done = i - 3
+            if 0 <= done < TILES - 2 and done % 2 == 1:
+                quantise_da(done - 1, 2)
+                if done % PER == PER - 1:
+                    product(done // PER)
+            if i >= TILES + 2 - 2:
+                quantise_da(i - 2, 1)
         product(E - 1)
 
         for m in range(2):
             one = held.tile([P, T], F32, name="one%d" % m, tag="plane%d" % (2 * m))
             two = held.tile([P, T], F32, name="two%d" % m, tag="plane%d" % (2 * m + 1))
-            for h in range(2):
-                cols = slice(h * 768, (h + 1) * 768)
-                lists = slice(h * 48, (h + 1) * 48)
-                nc.vector.tensor_copy(one[:, cols], dx[m][:].indirect(first[:, lists]))
-                nc.vector.tensor_copy(two[:, cols], dx[m][:].indirect(second[:, lists]))
-                total = ring2.tile([P, 768], F32, name="total")
+            cut = [0, 768, 1536] if m == 0 else [0, 1024, 1536]
+            for lo, hi in zip(cut, cut[1:]):
+                cols = slice(lo, hi)
+                nc.vector.tensor_copy(one[:, cols], dx[m][:].indirect(first[:, lo // 16 : hi // 16]))
+                nc.vector.tensor_copy(two[:, cols], dx[m][:].indirect(second[:, lo // 16 : hi // 16]))
+                total = ring2.tile([P, hi - lo], F32, name="total", tag="y")
                 adder = nc.gpsimd if m == 0 else nc.vector
                 adder.tensor_tensor(total[:], one[:, cols], two[:, cols], ADD)
                 nc.sync.dma_start(out[m * P : (m + 1) * P, cols], total[:])

@@ -22,6 +22,7 @@ SILU = mybir.ActivationFunctionType.Silu
 COPY = mybir.ActivationFunctionType.Copy
 
 P = 128
+AGAIN = [2, 9, 11, 15, 16, 17, 17, 21, 24, 24, 26, 28, 29, 32, 35, 39, 44]
 TILES = S // P
 PER = C // P
 
@@ -39,8 +40,8 @@ def tile_moe_bdx_mlp_silu_kernel(
         ring4 = ctx.enter_context(tc.tile_pool(name="ring4", bufs=4))
         ps_a = ctx.enter_context(tc.psum_pool(name="ps_a", bufs=2))
         ps_h = ctx.enter_context(tc.psum_pool(name="ps_h", bufs=3))
-        ps_t = ctx.enter_context(tc.psum_pool(name="ps_t", bufs=2))
-        ps_x = ctx.enter_context(tc.psum_pool(name="ps_x", bufs=1))
+        ps_t = ctx.enter_context(tc.psum_pool(name="ps_t", bufs=1))
+        ps_x = ctx.enter_context(tc.psum_pool(name="ps_x", bufs=2))
 
         offsets = held.tile([P, S // 16], U16, name="offsets")
         nc.sync.dma_start(offsets[:], offs)
@@ -107,9 +108,11 @@ def tile_moe_bdx_mlp_silu_kernel(
         load_w2(0)
         load_a_tile(1)
         load_a(1)
+        load_gate(2)
         load_w2(1)
         load_a(2)
         load_w1s()
+        load_gate(3)
         load_a(3)
         w1 = held.tile([P, E * 2, 2 * K], U8, name="w1", align_bytes=64)
         nc.sync.dma_start(w1[:].bitcast(I32), w1_words.rearrange("e s p k -> p (e s) k").bitcast(I32))
@@ -157,12 +160,11 @@ def tile_moe_bdx_mlp_silu_kernel(
         th = {}
         w = {}
 
-        def saved(i):
-            if i >= TILES:
-                return
-            th[i] = ring_s.tile([P, H], F32, name="th")
-            w[i] = ring_s.tile([P, H], F32, name="w")
-            for half in range(2):
+        def saved(i, half):
+            if half == 0:
+                th[i] = ring_s.tile([P, H], F32, name="th")
+                w[i] = ring_s.tile([P, H], F32, name="w")
+            if True:
                 cols = slice(half * 512, (half + 1) * 512)
                 bank = ps_a.tile([P, 512], F32, name="aT")
                 for b in range(4):
@@ -174,15 +176,17 @@ def tile_moe_bdx_mlp_silu_kernel(
         y = {}
         dh = {}
 
-        def hidden(i):
+        def hidden(i, half):
             if i >= TILES:
                 return
             e, c = i // PER, i % PER
-            dh[i] = []
-            for half in range(2):
+            if half == 0:
+                dh[i] = []
+            for again in range(1):
                 bank = ps_h.tile([P, 512], F32, name="dh")
                 dh[i].append(bank)
-                nc.tensor.matmul_mx(
+                for again in range(1 + AGAIN.count(2 * i + half)):
+                  nc.tensor.matmul_mx(
                     out=bank[:],
                     lhsT=g_codes[e][:, c * P : (c + 1) * P].bitcast(E5X4),
                     lhsT_scale=g_scales[e][:, c * P : (c + 1) * P],
@@ -204,7 +208,15 @@ def tile_moe_bdx_mlp_silu_kernel(
             if not 0 <= i < TILES:
                 return
             da[i] = ring4.tile([P, H], BF16, name="da", align_bytes=64)
-            nc.vector.scalar_tensor_tensor(out=da[i][:], in0=th[i][:], scalar=1.0, in1=y[i][:], op0=ADD, op1=MULT)
+            for u in range(2):
+                nc.vector.scalar_tensor_tensor(
+                    out=da[i][:].rearrange("p (g u q e) -> p u g q e", g=2, u=2, e=2)[:, u],
+                    in0=th[i][:].rearrange("p (g q u e) -> p u g q e", g=2, u=2, e=2)[:, u],
+                    scalar=1.0,
+                    in1=y[i][:].rearrange("p (g q u e) -> p u g q e", g=2, u=2, e=2)[:, u],
+                    op0=ADD,
+                    op1=MULT,
+                )
 
         da_t = {}
 
@@ -218,7 +230,7 @@ def tile_moe_bdx_mlp_silu_kernel(
             for g in range(2):
                 for u in range(2):
                     q = 2 * g + u
-                    nc.tensor.transpose(bank[:, q * P : (q + 1) * P], words[:, 256 * g + u : 256 * (g + 1) : 2], ident[:])
+                    nc.tensor.transpose(bank[:, q * P : (q + 1) * P], words[:, q * P : (q + 1) * P], ident[:])
             half = (i % 2) * P
             nc.scalar.copy(
                 da_t[i // 2][:].bitcast(F32).rearrange("p g (s u) -> p g s u", u=2)[:, :, half : half + P, :],
@@ -242,8 +254,8 @@ def tile_moe_bdx_mlp_silu_kernel(
                     in_=da_t[i // 2][:, g, 4 * half : 4 * (half + tiles * P)],
                 )
 
-        def product(e):
-            for m in range(2):
+        def product(e, m):
+            if True:
                 bank = ps_x.tile([P, C], F32, name="dxT")
                 for g in range(2):
                     nc.tensor.matmul_mx(
@@ -257,42 +269,78 @@ def tile_moe_bdx_mlp_silu_kernel(
                     )
                 nc.scalar.activation(dx[m][:, e * C : (e + 1) * C], bank[:], COPY, scale=-0.5)
 
-        for j in range(4):
-            gather(0, j)
-        for q in range(4):
-            interleave(0, q * P, (q + 1) * P)
-            quantise_g(0, q * P, (q + 1) * P)
-        saved(0)
-        hidden(0)
-        for i in range(1, 3):
-            saved(i)
+        gather(0, 0)
+        gather(1, 0)
+        gather(1, 1)
+        gather(0, 2)
+        gather(0, 1)
+        gather(0, 3)
+        load_a(2)
+        saved(0, 0)
+        saved(0, 1)
+        interleave(0, 0 * P, 1 * P)
+        interleave(0, 1 * P, 2 * P)
+        interleave(0, 3 * P, 4 * P)
+        quantise_g(0, 0 * P, 1 * P)
+        gather(1, 3)
+        interleave(0, 2 * P, 3 * P)
+        load_a(2)
+        saved(1, 0)
+        saved(1, 1)
+        gather(1, 2)
+        hidden(0, 0)
+        hidden(0, 1)
+        quantise_g(0, 3 * P, 4 * P)
+        quantise_g(0, 2 * P, 3 * P)
+        quantise_g(0, 1 * P, 2 * P)
+        ready = 4
         for i in range(TILES + 2):
             e, c = i // PER, i % PER
-            turn(i - 2)
-            load_a((i + 1) // 2 + 3)
-            saved(i + 3)
-            first_product(i)
             second_product(i - 1)
-            if e + 1 < E:
-                if c == 0:
-                    gather(e + 1, 0)
-                    gather(e + 1, 1)
-                elif c <= 2:
-                    gather(e + 1, c + 1)
-                if c >= 2:
-                    interleave(e + 1, (c - 2) * 256, (c - 1) * 256)
-                if c == 3:
-                    quantise_g(e + 1, 0, 256)
-                    quantise_g(e + 1, 256, 512)
-            hidden(i + 1)
+            done = i - 8
+            if 0 <= done < TILES - PER and done % PER == PER - 1:
+                product(done // PER, 0)
+            turn(i - 2)
+            if c == 1 and e + 1 < E:
+                quantise_g(e + 1, 0, 256)
+            if c == 3 and e + 1 < E:
+                quantise_g(e + 1, 256, 512)
+            if c == 0 and e + 1 < E:
+                interleave(e + 1, 0, 256)
+            if c == 2 and e + 1 < E:
+                interleave(e + 1, 256, 512)
+            hidden(i + 1, 0)
+            hidden(i + 1, 1)
+            first_product(i)
+            if c == 0:
+                if e + 2 < E:
+                    gather(e + 2, 0)
+            if c == 1:
+                if e + 2 < E:
+                    gather(e + 2, 1)
+            if c == 2:
+                if e + 2 < E:
+                    gather(e + 2, 2)
+            if c == 3:
+                if e + 2 < E:
+                    gather(e + 2, 3)
+            for unused in range(4):
+                if ready < min(2 * (i + 3 + 1), 2 * TILES):
+                    load_a(ready // 4 + 2)
+                    saved(ready // 2, ready % 2)
+                    ready += 1
             done = i - 3
             if 0 <= done < TILES - 2 and done % 2 == 1:
                 quantise_da(done - 1, 2)
-                if done % PER == PER - 1:
-                    product(done // PER)
-            if i >= TILES + 2 - 2:
+            if i - 2 >= TILES - 2:
                 quantise_da(i - 2, 1)
-        product(E - 1)
+            done = i - 8
+            if 0 <= done < TILES - PER and done % PER == PER - 1:
+                product(done // PER, 1)
+        product(4, 0)
+        product(4, 1)
+        product(E - 1, 0)
+        product(E - 1, 1)
 
         for m in range(2):
             one = held.tile([P, T], F32, name="one%d" % m, tag="plane%d" % (2 * m))

@@ -22,7 +22,7 @@ SILU = mybir.ActivationFunctionType.Silu
 COPY = mybir.ActivationFunctionType.Copy
 
 P = 128
-AGAIN = [2, 9, 11, 15, 16, 17, 17, 21, 24, 24, 26, 28, 29, 32, 35, 39, 44]
+AGAIN = [7, 9, 11, 13, 15, 17, 19, 21, 23, 25, 27, 29, 31, 33, 35, 37, 39]
 TILES = S // P
 PER = C // P
 
@@ -33,15 +33,15 @@ def tile_moe_bdx_mlp_silu_kernel(
     nc = tc.nc
     with ExitStack() as ctx:
         held = ctx.enter_context(tc.tile_pool(name="held", bufs=1))
-        ring_a = ctx.enter_context(tc.tile_pool(name="ring_a", bufs=3))
-        ring_s = ctx.enter_context(tc.tile_pool(name="ring_s", bufs=5))
+        ring_a = ctx.enter_context(tc.tile_pool(name="ring_a", bufs=4))
+        ring_s = ctx.enter_context(tc.tile_pool(name="ring_s", bufs=4))
         ring2 = ctx.enter_context(tc.tile_pool(name="ring2", bufs=2))
         ring3 = ctx.enter_context(tc.tile_pool(name="ring3", bufs=3))
         ring4 = ctx.enter_context(tc.tile_pool(name="ring4", bufs=4))
-        ps_a = ctx.enter_context(tc.psum_pool(name="ps_a", bufs=2))
+        ps_a = ctx.enter_context(tc.psum_pool(name="ps_a", bufs=3))
         ps_h = ctx.enter_context(tc.psum_pool(name="ps_h", bufs=3))
         ps_t = ctx.enter_context(tc.psum_pool(name="ps_t", bufs=1))
-        ps_x = ctx.enter_context(tc.psum_pool(name="ps_x", bufs=2))
+        ps_x = ctx.enter_context(tc.psum_pool(name="ps_x", bufs=1))
 
         offsets = held.tile([P, S // 16], U16, name="offsets")
         nc.sync.dma_start(offsets[:], offs)
@@ -61,12 +61,18 @@ def tile_moe_bdx_mlp_silu_kernel(
         w1s_rows = w1_scales.rearrange("e s f k -> f (e s) k").bitcast(I32)
         dy = {}
         gates = {}
+        pair_gate = {}
+        a_first = []
         a_tiles = {}
         w2 = {}
 
-        def load_gate(e):
-            gates[e] = held.tile([P, C], F32, name="gate%d" % e)
-            nc.sync.dma_start(gates[e][:], gate[0:P, e * C : (e + 1) * C])
+        def load_gate(q, lo, hi):
+            if lo == 0:
+                tile = held.tile([P, 2 * C], F32, name="gate%d" % q)
+                gates[2 * q] = tile[:, 0:C]
+                gates[2 * q + 1] = tile[:, C : 2 * C]
+                pair_gate[q] = tile
+            nc.sync.dma_start(pair_gate[q][:, lo:hi], gate[0:P, q * 2 * C + lo : q * 2 * C + hi])
 
         def load_dy(j):
             dy[j] = held.tile([P, T], F32, name="dy%d" % j, tag="plane%d" % j)
@@ -80,10 +86,13 @@ def tile_moe_bdx_mlp_silu_kernel(
             a_tiles[2 * h] = tile[:, :, 0:P]
             a_tiles[2 * h + 1] = tile[:, :, P : 2 * P]
 
-        def load_a_tile(i):
-            tile = held.tile([P, 8, P], F32, name="a_tile%d" % i)
-            nc.sync.dma_start(tile[:], a_rows[:, :, i * P : (i + 1) * P])
-            a_tiles[i] = tile[:]
+        def load_a_half(half):
+            if half == 0:
+                a_first.append(ring_a.tile([P, 8, 2 * P], F32, name="a_half"))
+                a_tiles[0] = a_first[0][:, :, 0:P]
+                a_tiles[1] = a_first[0][:, :, P : 2 * P]
+            rows = slice(4 * half, 4 * half + 4)
+            nc.sync.dma_start(a_first[0][:, rows, :], a_rows[:, rows, 0 : 2 * P])
 
         def load_w2(e):
             w2[e] = held.tile([P, 2 * H], U8, name="w2_%d" % e, align_bytes=64)
@@ -91,36 +100,34 @@ def tile_moe_bdx_mlp_silu_kernel(
 
         def load_w2s():
             for q in range(4):
-                nc.sync.dma_start(w2s[32 * q : 32 * q + 4].bitcast(I32), w2s_rows[4 * q : 4 * q + 4])
+                nc.scalar.dma_start(w2s[32 * q : 32 * q + 4].bitcast(I32), w2s_rows[4 * q : 4 * q + 4])
 
         def load_w1s():
             for q in range(4):
-                nc.sync.dma_start(w1s[32 * q : 32 * q + 4].bitcast(I32), w1s_rows[4 * q : 4 * q + 4])
+                nc.scalar.dma_start(w1s[32 * q : 32 * q + 4].bitcast(I32), w1s_rows[4 * q : 4 * q + 4])
 
-        load_gate(0)
+        load_w2s()
+        load_w1s()
+        load_gate(0, 0, C)
         load_dy(0)
-        load_gate(1)
+        load_gate(0, C, 2 * C)
         load_dy(1)
-        load_a_tile(0)
         load_dy(2)
         load_dy(3)
-        load_w2s()
         load_w2(0)
-        load_a_tile(1)
+        load_a_half(0)
+        load_a_half(1)
         load_a(1)
-        load_gate(2)
-        load_w2(1)
+        load_gate(1, 0, 2 * C)
         load_a(2)
-        load_w1s()
-        load_gate(3)
-        load_a(3)
+        load_w2(1)
         w1 = held.tile([P, E * 2, 2 * K], U8, name="w1", align_bytes=64)
         nc.sync.dma_start(w1[:].bitcast(I32), w1_words.rearrange("e s p k -> p (e s) k").bitcast(I32))
         for e in range(E):
             if e not in w2:
                 load_w2(e)
-            if e not in gates:
-                load_gate(e)
+            if e % 2 == 0 and e not in gates:
+                load_gate(e // 2, 0, 2 * C)
         first = held.tile([P, T // 16], U16, name="first")
         nc.sync.dma_start(first[:], pos1)
         second = held.tile([P, T // 16], U16, name="second")
@@ -139,7 +146,7 @@ def tile_moe_bdx_mlp_silu_kernel(
             nc.vector.tensor_tensor(
                 g4[e][:, j, :],
                 dy[j][:].indirect(offsets[:, e * (C // 16) : (e + 1) * (C // 16)]),
-                gates[e][:],
+                gates[e],
                 MULT,
             )
 
@@ -161,6 +168,8 @@ def tile_moe_bdx_mlp_silu_kernel(
         w = {}
 
         def saved(i, half):
+            if i >= TILES:
+                return
             if half == 0:
                 th[i] = ring_s.tile([P, H], F32, name="th")
                 w[i] = ring_s.tile([P, H], F32, name="w")
@@ -196,11 +205,12 @@ def tile_moe_bdx_mlp_silu_kernel(
                     stop=True,
                 )
 
-        def first_product(i):
+        def first_product(i, half):
             if i >= TILES:
                 return
-            y[i] = ring2.tile([P, H], F32, name="y")
-            for half in range(2):
+            if half == 0:
+                y[i] = ring2.tile([P, H], F32, name="y")
+            if True:
                 cols = slice(half * 512, (half + 1) * 512)
                 nc.vector.scalar_tensor_tensor(out=y[i][:, cols], in0=w[i][:, cols], scalar=1.0, in1=dh[i][half][:], op0=SUB, op1=MULT)
 
@@ -254,10 +264,19 @@ def tile_moe_bdx_mlp_silu_kernel(
                     in_=da_t[i // 2][:, g, 4 * half : 4 * (half + tiles * P)],
                 )
 
-        def product(e, m):
+        dxb = {}
+
+        def product(e, m, g):
+            if e < 0:
+                return
+            if g == 0:
+                if e < E - 1:
+                    dxb[e, m] = ps_x.tile([P, C], F32, name="dxT")
+                else:
+                    dxb[e, m] = ps_h.tile([P, C], F32, name="dh")
+            bank = dxb[e, m]
             if True:
-                bank = ps_x.tile([P, C], F32, name="dxT")
-                for g in range(2):
+                if True:
                     nc.tensor.matmul_mx(
                         out=bank[:],
                         lhsT=w1[:, 2 * e + g, m * 256 : (m + 1) * 256].bitcast(E2X4),
@@ -267,80 +286,83 @@ def tile_moe_bdx_mlp_silu_kernel(
                         start=(g == 0),
                         stop=(g == 1),
                     )
+            if g == 1:
                 nc.scalar.activation(dx[m][:, e * C : (e + 1) * C], bank[:], COPY, scale=-0.5)
 
-        gather(0, 0)
         gather(1, 0)
-        gather(1, 1)
-        gather(0, 2)
-        gather(0, 1)
-        gather(0, 3)
         load_a(2)
         saved(0, 0)
-        saved(0, 1)
+        gather(0, 0)
+        gather(1, 1)
+        gather(0, 1)
+        gather(0, 2)
+        gather(0, 3)
         interleave(0, 0 * P, 1 * P)
+        load_a(2)
+        saved(0, 1)
         interleave(0, 1 * P, 2 * P)
-        interleave(0, 3 * P, 4 * P)
-        quantise_g(0, 0 * P, 1 * P)
+        quantise_g(0, 0, 256)
         gather(1, 3)
-        interleave(0, 2 * P, 3 * P)
         load_a(2)
         saved(1, 0)
+        interleave(0, 3 * P, 4 * P)
+        hidden(0, 0)
+        interleave(0, 2 * P, 3 * P)
+        quantise_g(0, 256, 512)
+        load_a(2)
         saved(1, 1)
         gather(1, 2)
-        hidden(0, 0)
         hidden(0, 1)
-        quantise_g(0, 3 * P, 4 * P)
-        quantise_g(0, 2 * P, 3 * P)
-        quantise_g(0, 1 * P, 2 * P)
         ready = 4
-        for i in range(TILES + 2):
+        for i in range(TILES + 1):
             e, c = i // PER, i % PER
-            second_product(i - 1)
-            done = i - 8
-            if 0 <= done < TILES - PER and done % PER == PER - 1:
-                product(done // PER, 0)
-            turn(i - 2)
-            if c == 1 and e + 1 < E:
-                quantise_g(e + 1, 0, 256)
-            if c == 3 and e + 1 < E:
-                quantise_g(e + 1, 256, 512)
-            if c == 0 and e + 1 < E:
+            for unused in range(1):
+                if ready < min(2 * (i + 1) + 2, 2 * TILES):
+                    load_a(ready // 4 + 2)
+                    saved(ready // 2, ready % 2)
+                    ready += 1
+            if 0 <= i - 1 < TILES:
+                second_product(i - 1)
+            if e + 1 < E and c == 1:
                 interleave(e + 1, 0, 256)
-            if c == 2 and e + 1 < E:
+            if e + 1 < E and c == 1:
                 interleave(e + 1, 256, 512)
+            k = i - 6
+            if k >= 0 and k // PER < E - 1:
+                product(k // PER, (k % PER) // 2, k % 2)
             hidden(i + 1, 0)
-            hidden(i + 1, 1)
-            first_product(i)
-            if c == 0:
+            if c == 2:
                 if e + 2 < E:
                     gather(e + 2, 0)
-            if c == 1:
                 if e + 2 < E:
                     gather(e + 2, 1)
-            if c == 2:
                 if e + 2 < E:
                     gather(e + 2, 2)
             if c == 3:
                 if e + 2 < E:
                     gather(e + 2, 3)
-            for unused in range(4):
-                if ready < min(2 * (i + 3 + 1), 2 * TILES):
+            first_product(i, 0)
+            hidden(i + 1, 1)
+            if e + 1 < E and c == 1:
+                quantise_g(e + 1, 0, C)
+            for unused in range(1):
+                if ready < min(2 * (i + 1) + 1, 2 * TILES):
                     load_a(ready // 4 + 2)
                     saved(ready // 2, ready % 2)
                     ready += 1
-            done = i - 3
-            if 0 <= done < TILES - 2 and done % 2 == 1:
+            first_product(i, 1)
+            turn(i - 1)
+            done = i - 2
+            if 0 <= done < TILES - PER and done % 2 == 1:
                 quantise_da(done - 1, 2)
-            if i - 2 >= TILES - 2:
-                quantise_da(i - 2, 1)
-            done = i - 8
-            if 0 <= done < TILES - PER and done % PER == PER - 1:
-                product(done // PER, 1)
-        product(4, 0)
-        product(4, 1)
-        product(E - 1, 0)
-        product(E - 1, 1)
+            if i - 1 == TILES - 2:
+                quantise_da(TILES - PER, 2)
+            if i - 1 >= TILES - 2:
+                quantise_da(i - 1, 1)
+        for k in range(19, TILES - PER):
+            product(k // PER, (k % PER) // 2, k % 2)
+        for k in range(4):
+            product(E - 1, k // 2, k % 2)
 
         for m in range(2):
             one = held.tile([P, T], F32, name="one%d" % m, tag="plane%d" % (2 * m))

from contextlib import ExitStack

import concourse.mybir as mybir
from concourse.masks import make_identity

K, T, E, C, H, N = 256, 1536, 6, 512, 1024, 512
S = E * C
FLOPS = 2 * S * N * H + 2 * S * H * K
BYTES = 4 * (N * T + H * S + 128 * S + K * T) + E * (N * H // 2 + N * H // 32 + H * K // 2 + H * K // 32) + 2 * 128 * (S + 2 * T) // 16

F32 = mybir.dt.float32
BF16 = mybir.dt.bfloat16
I32 = mybir.dt.int32
U32 = mybir.dt.uint32
U16 = mybir.dt.uint16
U8 = mybir.dt.uint8
E5X4 = mybir.dt.float8_e5m2_x4
E2X4 = mybir.dt.float4_e2m1fn_x4
MULT, ADD, SUB = mybir.AluOpType.mult, mybir.AluOpType.add, mybir.AluOpType.subtract
TANH = mybir.ActivationFunctionType.Tanh
SILU = mybir.ActivationFunctionType.Silu
COPY = mybir.ActivationFunctionType.Copy

P = 128
AGAIN = [7, 9, 11, 13, 15, 17, 19, 21, 23, 25, 27, 29, 31, 33, 35, 37, 39]
TILES = S // P
PER = C // P


def tile_moe_bdx_mlp_silu_kernel(
    tc, dyT, a, w2_words, w2_scales, w1_words, w1_scales, gate, offs, pos1, pos2, out
):
    nc = tc.nc
    with ExitStack() as ctx:
        held = ctx.enter_context(tc.tile_pool(name="held", bufs=1))
        ring_a = ctx.enter_context(tc.tile_pool(name="ring_a", bufs=4))
        ring_s = ctx.enter_context(tc.tile_pool(name="ring_s", bufs=4))
        ring2 = ctx.enter_context(tc.tile_pool(name="ring2", bufs=2))
        ring3 = ctx.enter_context(tc.tile_pool(name="ring3", bufs=3))
        ring4 = ctx.enter_context(tc.tile_pool(name="ring4", bufs=4))
        ps_a = ctx.enter_context(tc.psum_pool(name="ps_a", bufs=3))
        ps_h = ctx.enter_context(tc.psum_pool(name="ps_h", bufs=3))
        ps_t = ctx.enter_context(tc.psum_pool(name="ps_t", bufs=1))
        ps_x = ctx.enter_context(tc.psum_pool(name="ps_x", bufs=1))

        offsets = held.tile([P, S // 16], U16, name="offsets")
        nc.sync.dma_start(offsets[:], offs)
        warm = held.tile([P, 8], F32, name="warm")
        nc.vector.memset(warm[:], 0.0)
        nc.scalar.activation(warm[:], warm[:], SILU)
        w2s = held.tile([P, E, H], U8, name="w2s", align_bytes=64)
        w1s = held.tile([P, E * 2, K], U8, name="w1s", align_bytes=64)
        nc.gpsimd.memset(w2s[:].bitcast(I32), 0)
        nc.gpsimd.memset(w1s[:].bitcast(I32), 0)
        ident = held.tile([P, P], F32, name="ident")
        make_identity(nc, ident[:])

        dy_rows = dyT.rearrange("(p j) t -> p j t", j=4)
        a_rows = a.rearrange("(b p) s -> p b s", p=P)
        w2s_rows = w2_scales.rearrange("e s f i -> f (e s) i").bitcast(I32)
        w1s_rows = w1_scales.rearrange("e s f k -> f (e s) k").bitcast(I32)
        dy = {}
        gates = {}
        pair_gate = {}
        a_first = []
        a_tiles = {}
        w2 = {}

        def load_gate(q, lo, hi):
            if lo == 0:
                tile = held.tile([P, 2 * C], F32, name="gate%d" % q)
                gates[2 * q] = tile[:, 0:C]
                gates[2 * q + 1] = tile[:, C : 2 * C]
                pair_gate[q] = tile
            nc.sync.dma_start(pair_gate[q][:, lo:hi], gate[0:P, q * 2 * C + lo : q * 2 * C + hi])

        def load_dy(j):
            dy[j] = held.tile([P, T], F32, name="dy%d" % j, tag="plane%d" % j)
            nc.sync.dma_start(dy[j][:], dy_rows[:, j, :])

        def load_a(h):
            if 2 * h in a_tiles or h >= TILES // 2:
                return
            tile = ring_a.tile([P, 8, 2 * P], F32, name="a_half")
            nc.sync.dma_start(tile[:], a_rows[:, :, h * 2 * P : (h + 1) * 2 * P])
            a_tiles[2 * h] = tile[:, :, 0:P]
            a_tiles[2 * h + 1] = tile[:, :, P : 2 * P]

        def load_a_half(half):
            if half == 0:
                a_first.append(ring_a.tile([P, 8, 2 * P], F32, name="a_half"))
                a_tiles[0] = a_first[0][:, :, 0:P]
                a_tiles[1] = a_first[0][:, :, P : 2 * P]
            rows = slice(4 * half, 4 * half + 4)
            nc.sync.dma_start(a_first[0][:, rows, :], a_rows[:, rows, 0 : 2 * P])

        def load_w2(e):
            w2[e] = held.tile([P, 2 * H], U8, name="w2_%d" % e, align_bytes=64)
            nc.sync.dma_start(w2[e][:].bitcast(I32), w2_words[e, 0].bitcast(I32))

        def load_w2s():
            for q in range(4):
                nc.scalar.dma_start(w2s[32 * q : 32 * q + 4].bitcast(I32), w2s_rows[4 * q : 4 * q + 4])

        def load_w1s():
            for q in range(4):
                nc.scalar.dma_start(w1s[32 * q : 32 * q + 4].bitcast(I32), w1s_rows[4 * q : 4 * q + 4])

        load_w2s()
        load_w1s()
        load_gate(0, 0, C)
        load_dy(0)
        load_gate(0, C, 2 * C)
        load_dy(1)
        load_dy(2)
        load_dy(3)
        load_w2(0)
        load_a_half(0)
        load_a_half(1)
        load_a(1)
        load_gate(1, 0, 2 * C)
        load_a(2)
        load_w2(1)
        w1 = held.tile([P, E * 2, 2 * K], U8, name="w1", align_bytes=64)
        nc.sync.dma_start(w1[:].bitcast(I32), w1_words.rearrange("e s p k -> p (e s) k").bitcast(I32))
        for e in range(E):
            if e not in w2:
                load_w2(e)
            if e % 2 == 0 and e not in gates:
                load_gate(e // 2, 0, 2 * C)
        first = held.tile([P, T // 16], U16, name="first")
        nc.sync.dma_start(first[:], pos1)
        second = held.tile([P, T // 16], U16, name="second")
        nc.sync.dma_start(second[:], pos2)

        dx = [held.tile([P, S], F32, name="dx%d" % m) for m in range(2)]

        g4 = {}
        g_bf = {}
        g_codes = {}
        g_scales = {}

        def gather(e, j):
            if j == 0:
                g4[e] = ring2.tile([P, 4, C], F32, name="g4")
            nc.vector.tensor_tensor(
                g4[e][:, j, :],
                dy[j][:].indirect(offsets[:, e * (C // 16) : (e + 1) * (C // 16)]),
                gates[e],
                MULT,
            )

        def interleave(e, lo, hi):
            if lo == 0:
                g_bf[e] = ring2.tile([P, 4 * C], BF16, name="g_bf", align_bytes=64)
            nc.scalar.copy(
                g_bf[e][:, 4 * lo : 4 * hi].rearrange("p (c i t) -> p c t i", i=4, t=4),
                g4[e][:, :, lo:hi].rearrange("p t (c i) -> p c t i", i=4),
            )

        def quantise_g(e, lo, hi):
            if lo == 0:
                g_codes[e] = ring2.tile([P, C], U32, name="g_codes", align_bytes=64)
                g_scales[e] = ring2.tile([P, C], U8, name="g_scales", align_bytes=64)
            nc.vector.quantize_mx(out=g_codes[e][:, lo:hi].bitcast(E5X4), scales=g_scales[e][:, lo:hi], in_=g_bf[e][:, 4 * lo : 4 * hi])

        th = {}
        w = {}

        def saved(i, half):
            if i >= TILES:
                return
            if half == 0:
                th[i] = ring_s.tile([P, H], F32, name="th")
                w[i] = ring_s.tile([P, H], F32, name="w")
            if True:
                cols = slice(half * 512, (half + 1) * 512)
                bank = ps_a.tile([P, 512], F32, name="aT")
                for b in range(4):
                    nc.tensor.transpose(bank[:, b * P : (b + 1) * P], a_tiles[i][:, half * 4 + b, :], ident[:])
                nc.scalar.activation(w[i][:, cols], bank[:], SILU, scale=-1.0)
                nc.scalar.activation(th[i][:, cols], bank[:], TANH, scale=0.5)

        da = {}
        y = {}
        dh = {}

        def hidden(i, half):
            if i >= TILES:
                return
            e, c = i // PER, i % PER
            if half == 0:
                dh[i] = []
            for again in range(1):
                bank = ps_h.tile([P, 512], F32, name="dh")
                dh[i].append(bank)
                for again in range(1 + AGAIN.count(2 * i + half)):
                  nc.tensor.matmul_mx(
                    out=bank[:],
                    lhsT=g_codes[e][:, c * P : (c + 1) * P].bitcast(E5X4),
                    lhsT_scale=g_scales[e][:, c * P : (c + 1) * P],
                    rhs=w2[e][:, half * 1024 : (half + 1) * 1024].bitcast(E2X4),
                    rhs_scale=w2s[:, e, half * 512 : (half + 1) * 512],
                    start=True,
                    stop=True,
                )

        def first_product(i, half):
            if i >= TILES:
                return
            if half == 0:
                y[i] = ring2.tile([P, H], F32, name="y")
            if True:
                cols = slice(half * 512, (half + 1) * 512)
                nc.vector.scalar_tensor_tensor(out=y[i][:, cols], in0=w[i][:, cols], scalar=1.0, in1=dh[i][half][:], op0=SUB, op1=MULT)

        def second_product(i):
            if not 0 <= i < TILES:
                return
            da[i] = ring4.tile([P, H], BF16, name="da", align_bytes=64)
            for u in range(2):
                nc.vector.scalar_tensor_tensor(
                    out=da[i][:].rearrange("p (g u q e) -> p u g q e", g=2, u=2, e=2)[:, u],
                    in0=th[i][:].rearrange("p (g q u e) -> p u g q e", g=2, u=2, e=2)[:, u],
                    scalar=1.0,
                    in1=y[i][:].rearrange("p (g q u e) -> p u g q e", g=2, u=2, e=2)[:, u],
                    op0=ADD,
                    op1=MULT,
                )

        da_t = {}

        def turn(i):
            if not 0 <= i < TILES:
                return
            if i % 2 == 0:
                da_t[i // 2] = ring3.tile([P, 2, 8 * P], BF16, name="da_t", align_bytes=64)
            words = da[i][:].bitcast(F32)
            bank = ps_t.tile([P, 512], F32, name="daT")
            for g in range(2):
                for u in range(2):
                    q = 2 * g + u
                    nc.tensor.transpose(bank[:, q * P : (q + 1) * P], words[:, q * P : (q + 1) * P], ident[:])
            half = (i % 2) * P
            nc.scalar.copy(
                da_t[i // 2][:].bitcast(F32).rearrange("p g (s u) -> p g s u", u=2)[:, :, half : half + P, :],
                bank[:].rearrange("p (g u s) -> p g s u", g=2, u=2),
            )

        d_codes = {}
        d_scales = {}

        def quantise_da(i, tiles):
            e, c = i // PER, i % PER
            if c == 0:
                d_codes[e] = ring2.tile([P, 2, C], U32, name="d_codes", align_bytes=64)
                d_scales[e] = ring2.tile([P, 2, C], U8, name="d_scales", align_bytes=64)
            cols = slice(c * P, (c + tiles) * P)
            half = (i % 2) * P
            for g in range(2):
                nc.vector.quantize_mx(
                    out=d_codes[e][:, g, cols].bitcast(E5X4),
                    scales=d_scales[e][:, g, cols],
                    in_=da_t[i // 2][:, g, 4 * half : 4 * (half + tiles * P)],
                )

        dxb = {}

        def product(e, m, g):
            if e < 0:
                return
            if g == 0:
                if e < E - 1:
                    dxb[e, m] = ps_x.tile([P, C], F32, name="dxT")
                else:
                    dxb[e, m] = ps_h.tile([P, C], F32, name="dh")
            bank = dxb[e, m]
            if True:
                if True:
                    nc.tensor.matmul_mx(
                        out=bank[:],
                        lhsT=w1[:, 2 * e + g, m * 256 : (m + 1) * 256].bitcast(E2X4),
                        lhsT_scale=w1s[:, 2 * e + g, m * P : (m + 1) * P],
                        rhs=d_codes[e][:, g, :].bitcast(E5X4),
                        rhs_scale=d_scales[e][:, g, :],
                        start=(g == 0),
                        stop=(g == 1),
                    )
            if g == 1:
                nc.scalar.activation(dx[m][:, e * C : (e + 1) * C], bank[:], COPY, scale=-0.5)

        gather(1, 0)
        load_a(2)
        saved(0, 0)
        gather(0, 0)
        gather(1, 1)
        gather(0, 1)
        gather(0, 2)
        gather(0, 3)
        interleave(0, 0 * P, 1 * P)
        load_a(2)
        saved(0, 1)
        interleave(0, 1 * P, 2 * P)
        quantise_g(0, 0, 256)
        gather(1, 3)
        load_a(2)
        saved(1, 0)
        interleave(0, 3 * P, 4 * P)
        hidden(0, 0)
        interleave(0, 2 * P, 3 * P)
        quantise_g(0, 256, 512)
        load_a(2)
        saved(1, 1)
        gather(1, 2)
        hidden(0, 1)
        ready = 4
        for i in range(TILES + 1):
            e, c = i // PER, i % PER
            for unused in range(1):
                if ready < min(2 * (i + 1) + 2, 2 * TILES):
                    load_a(ready // 4 + 2)
                    saved(ready // 2, ready % 2)
                    ready += 1
            if 0 <= i - 1 < TILES:
                second_product(i - 1)
            if e + 1 < E and c == 1:
                interleave(e + 1, 0, 256)
            if e + 1 < E and c == 1:
                interleave(e + 1, 256, 512)
            k = i - 6
            if k >= 0 and k // PER < E - 1:
                product(k // PER, (k % PER) // 2, k % 2)
            hidden(i + 1, 0)
            if c == 2:
                if e + 2 < E:
                    gather(e + 2, 0)
                if e + 2 < E:
                    gather(e + 2, 1)
                if e + 2 < E:
                    gather(e + 2, 2)
            if c == 3:
                if e + 2 < E:
                    gather(e + 2, 3)
            first_product(i, 0)
            hidden(i + 1, 1)
            if e + 1 < E and c == 1:
                quantise_g(e + 1, 0, C)
            for unused in range(1):
                if ready < min(2 * (i + 1) + 1, 2 * TILES):
                    load_a(ready // 4 + 2)
                    saved(ready // 2, ready % 2)
                    ready += 1
            first_product(i, 1)
            turn(i - 1)
            done = i - 2
            if 0 <= done < TILES - PER and done % 2 == 1:
                quantise_da(done - 1, 2)
            if i - 1 == TILES - 2:
                quantise_da(TILES - PER, 2)
            if i - 1 >= TILES - 2:
                quantise_da(i - 1, 1)
        for k in range(19, TILES - PER):
            product(k // PER, (k % PER) // 2, k % 2)
        for k in range(4):
            product(E - 1, k // 2, k % 2)

        for m in range(2):
            one = held.tile([P, T], F32, name="one%d" % m, tag="plane%d" % (2 * m))
            two = held.tile([P, T], F32, name="two%d" % m, tag="plane%d" % (2 * m + 1))
            cut = [0, 768, 1536] if m == 0 else [0, 1024, 1536]
            for lo, hi in zip(cut, cut[1:]):
                cols = slice(lo, hi)
                nc.vector.tensor_copy(one[:, cols], dx[m][:].indirect(first[:, lo // 16 : hi // 16]))
                nc.vector.tensor_copy(two[:, cols], dx[m][:].indirect(second[:, lo // 16 : hi // 16]))
                total = ring2.tile([P, hi - lo], F32, name="total", tag="y")
                adder = nc.gpsimd if m == 0 else nc.vector
                adder.tensor_tensor(total[:], one[:, cols], two[:, cols], ADD)
                nc.sync.dma_start(out[m * P : (m + 1) * P, cols], total[:])
